import numpy as np
import ml_dtypes


def mxq(x, axis, fmt="e4m3"):
    dtype, down = {"e4m3": (ml_dtypes.float8_e4m3fn, 7), "e5m2": (ml_dtypes.float8_e5m2, 14)}[fmt]
    v = np.moveaxis(np.asarray(x, np.float32).astype(ml_dtypes.bfloat16).astype(np.float64), axis, -1)
    blocks = v.reshape(v.shape[:-1] + (-1, 32))
    amax = np.abs(blocks).max(-1, keepdims=True)
    byte = np.maximum(np.where(amax > 0, np.frexp(amax)[1] - 1 + 127, 0) - down, 1)
    scale = np.exp2(byte - 127.0)
    codes = (blocks / scale).astype(np.float32).astype(dtype).astype(np.float64)
    return np.moveaxis((codes * scale).reshape(v.shape), -1, axis)


WIDE = False


def mx_kscale(k):
    if not WIDE:
        return np.ones(k)
    levels = np.array([10, -10, 5, -5, 0])
    if k % 512:
        return np.exp2(np.random.permutation(np.resize(levels, k // 32))).repeat(32)
    a = np.empty((k // 512, 16))
    for p in range(k // 512):
        a[p, :8] = np.random.permutation(np.resize(levels, 8))
        for g in range(8):
            far = levels[np.abs(levels - a[p, g]) >= 10]
            a[p, g + 8] = far[np.random.randint(len(far))]
    return np.exp2(a.ravel()).repeat(32)


def f64(x):
    return np.asarray(x).astype(np.float64)


def planes(y):
    n, m = y.shape
    v = y.astype(np.float32).astype(ml_dtypes.bfloat16).astype(np.float64).reshape(n // 32, 32, m)
    top = np.abs(v).max(1)
    byte = np.clip(np.where(top > 0, np.frexp(top)[1] - 1 + 127 - 7, 1), 1, 254)
    codes = (v * np.exp2(127.0 - byte)[:, None, :]).reshape(n, m).astype(np.float32).astype(ml_dtypes.float8_e4m3fn).view(np.uint8)
    words = codes.reshape(n // 512, 128, 4, m).transpose(0, 1, 3, 2)
    return np.ascontiguousarray(words), np.ascontiguousarray(byte.astype(np.uint8).reshape(n // 512, 16, m))


def split(x):
    m, e = np.frexp(f64(x))
    hi = np.ldexp(np.trunc(16.0 * m) / 16.0, e)
    return hi, f64(x) - hi


def gelu(v):
    return 0.5 * v * (1.0 + np.tanh(np.sqrt(2.0 / np.pi) * (v + 0.044715 * v**3)))


K, M, T = 512, 1024, 1536


def setup_inputs():
    n = np.random.standard_normal
    s = mx_kscale(K)[:, None]
    return {
        "w": (n((K, M)) / np.sqrt(K) / s).astype(np.float32),
        "x": (n((K, T)) * s).astype(np.float32),
        "b": (0.3 * n(1024)).astype(np.float32),
    }


def reference(w, x, b):
    w_hi, w_lo = split(w)
    w_hi_, w_lo_ = mxq(w_hi, 0, "e4m3"), mxq(w_lo, 0, "e4m3")
    x_hi, x_lo = split(x)
    x_hi_, x_lo_ = mxq(x_hi, 0, "e4m3"), mxq(x_lo, 0, "e4m3")
    y = w_hi_.T @ x_hi_ + w_hi_.T @ x_lo_ + w_lo_.T @ x_hi_
    out_0 = gelu(y + f64(b)[:, None])
    return (out_0,) + planes(out_0)

@@ -1,0 +1,160 @@
+from contextlib import ExitStack
+
+import concourse.mybir as mybir
+
+K, M, T = 512, 1024, 1536
+FLOPS = 3 * 2 * K * M * T
+
+F32 = mybir.dt.float32
+BF16 = mybir.dt.bfloat16
+I32 = mybir.dt.int32
+U32 = mybir.dt.uint32
+U8 = mybir.dt.uint8
+FP8X4 = mybir.dt.float8_e4m3fn_x4
+GELU = mybir.ActivationFunctionType.Gelu_apprx_tanh
+
+P = 128
+MASK = -983056
+XUN = [128, 128, 256, 256, 256, 256, 256]
+CHUNKS = [(0, 512), (512, 256), (768, 256), (1024, 256), (1280, 256)]
+EXV = ['x0']
+SIL = ['40']
+SCAL = [(0, 4), (4, 5)]
+ORDER = 'Lx0 Lx1 Lx2 Lw0 Ex0 Ex1 Ax0 Hx0 Cx0 Lw1 Ex2 Ax1 Ox0 Hx1 Ax2 Cx1 Lx3 Hx2 Ew00 Ox1 Lx4 Ew01 Aw00 Cx2 Lx5 Ew10 Hw00 Ox2 Lx6 Aw01 Ew11 Cw00 Ex3 Hw01 Ow00 Aw10 M000 Cw01 M001 G000 Hw10 Ow01 G001 Aw11 M002 Cw10 Ex4 Z000 M003 Hw11 G002 Ow10 Ax3 G003 M010 Cw11 Ex5 Z001 M011 Hx3 Ow11 G010 Ax4 M012 Cx3 G011 M013 Ex6 Z010 Hx4 Ox3 Ax5 G012 M100 Cx4 M101 G013 M102 G100 M103 Z011 Hx5 G101 Ox4 M110 G102 Ax6 M111 G103 Cx5 Z100 G110 M112 G111 M113 Z101 G112 M200 Hx6 G113 Z110 Ox5 M201 G200 Cx6 Z111 M202 G201 M203 G202 Z200 M210 G203 Ox6 M211 G210 Z201 I00 M212 G211 M213 G212 Z210 M300 G213 I01 M301 G300 Z211 M302 G301 M303 G302 Z300 Q00 M310 G303 I10 M311 Y00 G310 M312 G311 Q01 Z301 M313 G312 I11 Z310 M400 G313 M401 Y01 G400 Q10 M402 I20 G401 Z311 M403 G402 Q11 Y10 M410 G403 I21 Z400 M411 G410 Q20 Y11 M412 G411 I30 Z401 M413 G412 Y20 Q21 G413 Z410 I31 I40 Y21 Q30 Z411 Q31 I41 Y30 Y31 Q40 X0 Q41 Y40 Y41 X1'
+
+
+def tile_mix_split3_fm_pl_gelu_kernel(tc, w, x, b, out_0, out_1, out_2):
+    nc = tc.nc
+    with ExitStack() as ctx:
+        keep = ctx.enter_context(tc.tile_pool(name="keep", bufs=1))
+        psum = ctx.enter_context(tc.psum_pool(name="psum", bufs=8))
+        ctx.enter_context(tc.manual_schedule())
+
+        xv = x.rearrange("(p j) t -> p j t", j=4)
+        wv = w.rearrange("(p j) n -> p j n", j=4)
+        o0 = out_0.rearrange("(a p r) t -> a p r t", a=2, r=4)
+        o1 = out_1.rearrange("a p t i -> a p (t i)").bitcast(I32)
+        o2 = out_2.bitcast(I32)
+
+        codes = {}
+        scales = {}
+        for side, width in (("x", T), ("w", M)):
+            for part in "HO":
+                codes[side + part] = keep.tile([P, width], U32, align_bytes=64, name="codes_" + side + part)
+                scales[side + part] = keep.tile([P, width], U8, align_bytes=64, name="scales_" + side + part)
+        oscale = keep.tile([P, T], U8, align_bytes=64)
+        bias = keep.tile([P, 2, 4], F32)
+        warm = keep.tile([P, 8], F32)
+        warm_out = keep.tile([P, 8], F32)
+
+        nc.gpsimd.memset(warm[:], 0.0)
+        nc.scalar.activation(out=warm_out[:, 0:1], in_=warm[:, 0:1], func=GELU)
+        nc.gpsimd.dma_start(out=bias[:], in_=b.rearrange("(a p r) -> p a r", a=2, r=4))
+
+        xstart = [sum(XUN[:i]) for i in range(len(XUN))]
+        raw, hi, lo, acc, res, obf, owords = {}, {}, {}, {}, {}, {}, {}
+
+        def width_of(u):
+            return XUN[int(u[1])] if u[0] == "x" else 256
+
+        def first_col(u):
+            return xstart[int(u[1])] if u[0] == "x" else 512 * int(u[1]) + 256 * int(u[2])
+
+        def src_view(u, upper):
+            t = raw[u[:2]][:]
+            if upper:
+                t = t.bitcast(BF16)[:, :, 1::2]
+            if u[0] == "x":
+                return t.rearrange("p j (c i) -> p c j i", i=2)
+            h = int(u[2])
+            return t.rearrange("p j (m r) -> p m j r", r=4)[:, :, :, 2 * h : 2 * h + 2]
+
+        def dst_view(u, t):
+            if u[0] == "x":
+                return t[:].rearrange("p (c i j) -> p c j i", i=2, j=4)
+            return t[:].rearrange("p (r m j) -> p m j r", r=2, j=4)
+
+        for task in ORDER.split():
+            kind, u = task[0], task[1:]
+            if kind == "L":
+                if u[0] == "x":
+                    wd, c0 = width_of(u), first_col(u)
+                    raw[u] = keep.tile([P, 4, wd], F32, name="raw_" + u, align_bytes=64)
+                    nc.sync.dma_start(out=raw[u][:], in_=xv[:, :, c0 : c0 + wd])
+                else:
+                    a = int(u[1])
+                    raw[u] = keep.tile([P, 4, 512], F32, name="raw_" + u, align_bytes=64)
+                    nc.sync.dma_start(out=raw[u][:], in_=wv[:, :, 512 * a : 512 * a + 512])
+            elif kind == "E":
+                hi[u] = keep.tile([P, 4 * width_of(u)], BF16, name="hi_" + u, align_bytes=64)
+                if u in EXV:
+                    nc.vector.tensor_copy(out=dst_view(u, hi[u]), in_=src_view(u, True))
+                else:
+                    nc.scalar.copy(out=dst_view(u, hi[u]), in_=src_view(u, True))
+            elif kind == "A":
+                nc.vector.tensor_scalar(
+                    out=hi[u][:].bitcast(I32), in0=hi[u][:].bitcast(I32), scalar1=MASK, scalar2=None,
+                    op0=mybir.AluOpType.bitwise_and,
+                )
+            elif kind == "C":
+                lo[u] = keep.tile([P, 4 * width_of(u)], BF16, name="lo_" + u, align_bytes=64)
+                nc.vector.tensor_tensor(
+                    out=dst_view(u, lo[u]), in0=src_view(u, False), in1=dst_view(u, hi[u]),
+                    op=mybir.AluOpType.subtract,
+                )
+            elif kind in "HO":
+                cols = slice(first_col(u), first_col(u) + width_of(u))
+                nc.vector.quantize_mx(
+                    out=codes[u[0] + kind][:, cols].bitcast(FP8X4), scales=scales[u[0] + kind][:, cols],
+                    in_=(hi if kind == "H" else lo)[u][:],
+                )
+            elif kind == "M":
+                c0, n = CHUNKS[int(u[0])]
+                a, r = int(u[1]), int(u[2])
+                bank = psum.tile([P, 512], F32, name="bank")
+                acc[u] = bank
+                mc = slice(512 * a + 128 * r, 512 * a + 128 * r + 128)
+                ncol = slice(c0, c0 + n)
+                for i, (pw, px) in enumerate((("wH", "xH"), ("wH", "xO"), ("wO", "xH"))):
+                    nc.tensor.matmul_mx(
+                        out=bank[:, 0:n], lhsT=codes[pw][:, mc].bitcast(FP8X4), lhsT_scale=scales[pw][:, mc],
+                        rhs=codes[px][:, ncol].bitcast(FP8X4), rhs_scale=scales[px][:, ncol],
+                        start=(i == 0), stop=(i == 2),
+                    )
+            elif kind == "G":
+                c0, n = CHUNKS[int(u[0])]
+                a, r = int(u[1]), int(u[2])
+                if u[:2] not in res:
+                    res[u[:2]] = keep.tile([P, 4, n], F32, name="res_" + u[:2], align_bytes=64)
+                nc.scalar.activation(out=res[u[:2]][:, r, :], in_=acc[u][:, 0:n], func=GELU, bias=bias[:, a, r : r + 1])
+            elif kind == "Z":
+                c0, n = CHUNKS[int(u[0])]
+                a, h = int(u[1]), int(u[2])
+                nc.sync.dma_start(out=o0[a, :, 2 * h : 2 * h + 2, c0 : c0 + n], in_=res[u[:2]][:, 2 * h : 2 * h + 2, :])
+            elif kind == "I":
+                c0, n = CHUNKS[int(u[0])]
+                obf[u] = keep.tile([P, 4 * n], BF16, name="obf_" + u, align_bytes=64)
+                dst = obf[u][:].rearrange("p (c i r) -> p c r i", i=2, r=4)
+                src = res[u][:].rearrange("p r (c i) -> p c r i", i=2)
+                if u in SIL:
+                    nc.scalar.copy(out=dst, in_=src)
+                else:
+                    nc.vector.tensor_copy(out=dst, in_=src)
+            elif kind == "Q":
+                c0, n = CHUNKS[int(u[0])]
+                a = int(u[1])
+                owords[u] = keep.tile([P, n], U32, name="owords_" + u, align_bytes=64)
+                nc.vector.quantize_mx(
+                    out=owords[u][:].bitcast(FP8X4), scales=oscale[4 * a : P, c0 : c0 + n], in_=obf[u][:]
+                )
+            elif kind == "Y":
+                c0, n = CHUNKS[int(u[0])]
+                nc.sync.dma_start(out=o1[int(u[1]), :, c0 : c0 + n], in_=owords[u][:].bitcast(I32))
+            else:
+                k0, k1 = SCAL[int(u)]
+                c0, c1 = CHUNKS[k0][0], CHUNKS[k1 - 1][0] + CHUNKS[k1 - 1][1]
+                for q in range(4):
+                    nc.sync.dma_start(
+                        out=o2[:, 4 * q : 4 * q + 4, c0 // 4 : c1 // 4],
+                        in_=oscale[32 * q : 32 * q + 8, c0:c1].bitcast(I32),
+                    )

@@ -16,11 +16,13 @@ GELU = mybir.ActivationFunctionType.Gelu_apprx_tanh
 P = 128
 MASK = -983056
 XUN = [128, 128, 256, 256, 256, 256, 256]
-CHUNKS = [(0, 512), (512, 256), (768, 256), (1024, 256), (1280, 256)]
-EXV = ['x0']
-SIL = ['40']
-SCAL = [(0, 4), (4, 5)]
-ORDER = 'Lx0 Lx1 Lx2 Lw0 Ex0 Ex1 Ax0 Hx0 Cx0 Lw1 Ex2 Ax1 Ox0 Hx1 Ax2 Cx1 Lx3 Hx2 Ew00 Ox1 Lx4 Ew01 Aw00 Cx2 Lx5 Ew10 Hw00 Ox2 Lx6 Aw01 Ew11 Cw00 Ex3 Hw01 Ow00 Aw10 M000 Cw01 M001 G000 Hw10 Ow01 G001 Aw11 M002 Cw10 Ex4 Z000 M003 Hw11 G002 Ow10 Ax3 G003 M010 Cw11 Ex5 Z001 M011 Hx3 Ow11 G010 Ax4 M012 Cx3 G011 M013 Ex6 Z010 Hx4 Ox3 Ax5 G012 M100 Cx4 M101 G013 M102 G100 M103 Z011 Hx5 G101 Ox4 M110 G102 Ax6 M111 G103 Cx5 Z100 G110 M112 G111 M113 Z101 G112 M200 Hx6 G113 Z110 Ox5 M201 G200 Cx6 Z111 M202 G201 M203 G202 Z200 M210 G203 Ox6 M211 G210 Z201 I00 M212 G211 M213 G212 Z210 M300 G213 I01 M301 G300 Z211 M302 G301 M303 G302 Z300 Q00 M310 G303 I10 M311 Y00 G310 M312 G311 Q01 Z301 M313 G312 I11 Z310 M400 G313 M401 Y01 G400 Q10 M402 I20 G401 Z311 M403 G402 Q11 Y10 M410 G403 I21 Z400 M411 G410 Q20 Y11 M412 G411 I30 Z401 M413 G412 Y20 Q21 G413 Z410 I31 I40 Y21 Q30 Z411 Q31 I41 Y30 Y31 Q40 X0 Q41 Y40 Y41 X1'
+CHUNKS = [(0, 512), (512, 512), (1024, 512)]
+XLD = [(0, 256), (256, 256), (512, 512), (1024, 512)]
+SEGS = [(0, 512), (512, 512), (1024, 512)]
+EXV = ['x0', 'x1']
+SIL = ['21']
+SCAL = [(0, 1), (1, 3)]
+ORDER = 'Lx0 Lx1 Lw0 Ex0 Ex1 Ax0 Ax1 Cx0 Lx2 Ex2 Cx1 Hx0 Ox0 Ax2 Ox1 Cx2 Lw1 Ew00 Hx2 Ox2 Ew01 Aw00 Hx1 Hw00 Cw00 Lx3 M0000 Ex3 M0010 M0011 M0001 Aw01 Ex4 Ow00 Cw01 M0002 M0012 Ew11 Hw01 Ow01 M0031 Ax4 M0020 G001 Ax3 M0032 Hx4 M0022 G000 Hx3 M0030 M0021 Aw11 M1010 G003 Cx4 Z000 M1000 M1030 Ex6 M1032 M1002 Hw11 M1012 M1022 Cw11 G002 M1120 M0130 M0120 Ew10 Z001 M0121 Ox4 M0131 Ow11 M1130 Cx3 M1020 Ex5 M0132 M0122 M1132 M1122 Aw10 G013 Ox3 Cw10 M1001 G012 M1121 M1131 G100 Z011 M1011 Hw10 M1021 G101 M1031 Ow10 Ax5 G103 Ax6 M1101 Z100 M0111 Cx5 G102 M0112 M0102 G113 M0101 Z101 M1102 Cx6 G112 M1110 M0110 M1111 G011 Z111 M0100 M1112 Ox5 G010 M1100 Ox6 Hx5 G110 M2011 Hx6 Z010 M2021 I01 M2001 G111 M2002 M2000 Z110 M2010 G200 M2012 I11 M2101 G201 M2032 M2022 M2020 Z200 M2100 Q01 G202 M2031 M2111 Q11 M2030 M2112 Y01 I00 G203 M2102 M2122 Y11 G210 M2110 M2131 Z201 M2130 G211 I20 M2120 M2132 M2121 G213 Z210 Q00 G212 Q20 I21 X0 I10 Y00 Y20 Z211 Q10 Q21 Y10 Y21 X1'
 
 
 def tile_mix_split3_fm_pl_gelu_kernel(tc, w, x, b, out_0, out_1, out_2):
@@ -47,11 +49,12 @@ def tile_mix_split3_fm_pl_gelu_kernel(tc, w, x, b, out_0, out_1, out_2):
         warm = keep.tile([P, 8], F32)
         warm_out = keep.tile([P, 8], F32)
 
-        nc.gpsimd.memset(warm[:], 0.0)
+        nc.vector.memset(warm[:], 0.0)
         nc.scalar.activation(out=warm_out[:, 0:1], in_=warm[:, 0:1], func=GELU)
-        nc.gpsimd.dma_start(out=bias[:], in_=b.rearrange("(a p r) -> p a r", a=2, r=4))
+        nc.scalar.dma_start(out=bias[:], in_=b.rearrange("(a p r) -> p a r", a=2, r=4))
 
         xstart = [sum(XUN[:i]) for i in range(len(XUN))]
+        done = {}
         raw, hi, lo, acc, res, obf, owords = {}, {}, {}, {}, {}, {}, {}
 
         def width_of(u):
@@ -61,7 +64,12 @@ def tile_mix_split3_fm_pl_gelu_kernel(tc, w, x, b, out_0, out_1, out_2):
             return xstart[int(u[1])] if u[0] == "x" else 512 * int(u[1]) + 256 * int(u[2])
 
         def src_view(u, upper):
-            t = raw[u[:2]][:]
+            if u[0] == "x":
+                c0 = first_col(u)
+                li = [i for i, (d0, wd) in enumerate(XLD) if d0 <= c0 < d0 + wd][0]
+                t = raw["x%d" % li][:, :, c0 - XLD[li][0] : c0 - XLD[li][0] + width_of(u)]
+            else:
+                t = raw[u[:2]][:]
             if upper:
                 t = t.bitcast(BF16)[:, :, 1::2]
             if u[0] == "x":
@@ -78,7 +86,7 @@ def tile_mix_split3_fm_pl_gelu_kernel(tc, w, x, b, out_0, out_1, out_2):
             kind, u = task[0], task[1:]
             if kind == "L":
                 if u[0] == "x":
-                    wd, c0 = width_of(u), first_col(u)
+                    c0, wd = XLD[int(u[1])]
                     raw[u] = keep.tile([P, 4, wd], F32, name="raw_" + u, align_bytes=64)
                     nc.sync.dma_start(out=raw[u][:], in_=xv[:, :, c0 : c0 + wd])
                 else:
@@ -111,16 +119,18 @@ def tile_mix_split3_fm_pl_gelu_kernel(tc, w, x, b, out_0, out_1, out_2):
             elif kind == "M":
                 c0, n = CHUNKS[int(u[0])]
                 a, r = int(u[1]), int(u[2])
-                bank = psum.tile([P, 512], F32, name="bank")
-                acc[u] = bank
+                if u[:3] not in acc:
+                    acc[u[:3]] = psum.tile([P, 512], F32, name="bank")
+                    done[u[:3]] = 0
                 mc = slice(512 * a + 128 * r, 512 * a + 128 * r + 128)
                 ncol = slice(c0, c0 + n)
-                for i, (pw, px) in enumerate((("wH", "xH"), ("wH", "xO"), ("wO", "xH"))):
-                    nc.tensor.matmul_mx(
-                        out=bank[:, 0:n], lhsT=codes[pw][:, mc].bitcast(FP8X4), lhsT_scale=scales[pw][:, mc],
-                        rhs=codes[px][:, ncol].bitcast(FP8X4), rhs_scale=scales[px][:, ncol],
-                        start=(i == 0), stop=(i == 2),
-                    )
+                pw, px = (("wH", "xH"), ("wH", "xO"), ("wO", "xH"))[int(u[3])]
+                nc.tensor.matmul_mx(
+                    out=acc[u[:3]][:, 0:n], lhsT=codes[pw][:, mc].bitcast(FP8X4), lhsT_scale=scales[pw][:, mc],
+                    rhs=codes[px][:, ncol].bitcast(FP8X4), rhs_scale=scales[px][:, ncol],
+                    start=(done[u[:3]] == 0), stop=(done[u[:3]] == 2),
+                )
+                done[u[:3]] += 1
             elif kind == "G":
                 c0, n = CHUNKS[int(u[0])]
                 a, r = int(u[1]), int(u[2])
@@ -132,27 +142,29 @@ def tile_mix_split3_fm_pl_gelu_kernel(tc, w, x, b, out_0, out_1, out_2):
                 a, h = int(u[1]), int(u[2])
                 nc.sync.dma_start(out=o0[a, :, 2 * h : 2 * h + 2, c0 : c0 + n], in_=res[u[:2]][:, 2 * h : 2 * h + 2, :])
             elif kind == "I":
-                c0, n = CHUNKS[int(u[0])]
+                c0, n = SEGS[int(u[0])]
+                ck = [i for i, (d0, wd) in enumerate(CHUNKS) if d0 <= c0 < d0 + wd][0]
+                d0 = c0 - CHUNKS[ck][0]
                 obf[u] = keep.tile([P, 4 * n], BF16, name="obf_" + u, align_bytes=64)
                 dst = obf[u][:].rearrange("p (c i r) -> p c r i", i=2, r=4)
-                src = res[u][:].rearrange("p r (c i) -> p c r i", i=2)
+                src = res["%d%s" % (ck, u[1])][:, :, d0 : d0 + n].rearrange("p r (c i) -> p c r i", i=2)
                 if u in SIL:
                     nc.scalar.copy(out=dst, in_=src)
                 else:
                     nc.vector.tensor_copy(out=dst, in_=src)
             elif kind == "Q":
-                c0, n = CHUNKS[int(u[0])]
+                c0, n = SEGS[int(u[0])]
                 a = int(u[1])
                 owords[u] = keep.tile([P, n], U32, name="owords_" + u, align_bytes=64)
                 nc.vector.quantize_mx(
                     out=owords[u][:].bitcast(FP8X4), scales=oscale[4 * a : P, c0 : c0 + n], in_=obf[u][:]
                 )
             elif kind == "Y":
-                c0, n = CHUNKS[int(u[0])]
+                c0, n = SEGS[int(u[0])]
                 nc.sync.dma_start(out=o1[int(u[1]), :, c0 : c0 + n], in_=owords[u][:].bitcast(I32))
             else:
                 k0, k1 = SCAL[int(u)]
-                c0, c1 = CHUNKS[k0][0], CHUNKS[k1 - 1][0] + CHUNKS[k1 - 1][1]
+                c0, c1 = SEGS[k0][0], SEGS[k1 - 1][0] + SEGS[k1 - 1][1]
                 for q in range(4):
                     nc.sync.dma_start(
                         out=o2[:, 4 * q : 4 * q + 4, c0 // 4 : c1 // 4],

from contextlib import ExitStack

import concourse.mybir as mybir

K, M, T = 512, 1024, 1536
FLOPS = 3 * 2 * K * M * T

F32 = mybir.dt.float32
BF16 = mybir.dt.bfloat16
I32 = mybir.dt.int32
U32 = mybir.dt.uint32
U8 = mybir.dt.uint8
FP8X4 = mybir.dt.float8_e4m3fn_x4
GELU = mybir.ActivationFunctionType.Gelu_apprx_tanh

P = 128
MASK = -983056
XUN = [128, 128, 256, 256, 256, 256, 256]
CHUNKS = [(0, 512), (512, 512), (1024, 512)]
XLD = [(0, 256), (256, 256), (512, 512), (1024, 512)]
SEGS = [(0, 512), (512, 512), (1024, 512)]
EXV = ['x0', 'x1']
SIL = ['21']
SCAL = [(0, 1), (1, 3)]
ORDER = 'Lx0 Lx1 Lw0 Ex0 Ex1 Ax0 Ax1 Cx0 Lx2 Ex2 Cx1 Hx0 Ox0 Ax2 Ox1 Cx2 Lw1 Ew00 Hx2 Ox2 Ew01 Aw00 Hx1 Hw00 Cw00 Lx3 M0000 Ex3 M0010 M0011 M0001 Aw01 Ex4 Ow00 Cw01 M0002 M0012 Ew11 Hw01 Ow01 M0031 Ax4 M0020 G001 Ax3 M0032 Hx4 M0022 G000 Hx3 M0030 M0021 Aw11 M1010 G003 Cx4 Z000 M1000 M1030 Ex6 M1032 M1002 Hw11 M1012 M1022 Cw11 G002 M1120 M0130 M0120 Ew10 Z001 M0121 Ox4 M0131 Ow11 M1130 Cx3 M1020 Ex5 M0132 M0122 M1132 M1122 Aw10 G013 Ox3 Cw10 M1001 G012 M1121 M1131 G100 Z011 M1011 Hw10 M1021 G101 M1031 Ow10 Ax5 G103 Ax6 M1101 Z100 M0111 Cx5 G102 M0112 M0102 G113 M0101 Z101 M1102 Cx6 G112 M1110 M0110 M1111 G011 Z111 M0100 M1112 Ox5 G010 M1100 Ox6 Hx5 G110 M2011 Hx6 Z010 M2021 I01 M2001 G111 M2002 M2000 Z110 M2010 G200 M2012 I11 M2101 G201 M2032 M2022 M2020 Z200 M2100 Q01 G202 M2031 M2111 Q11 M2030 M2112 Y01 I00 G203 M2102 M2122 Y11 G210 M2110 M2131 Z201 M2130 G211 I20 M2120 M2132 M2121 G213 Z210 Q00 G212 Q20 I21 X0 I10 Y00 Y20 Z211 Q10 Q21 Y10 Y21 X1'


def tile_mix_split3_fm_pl_gelu_kernel(tc, w, x, b, out_0, out_1, out_2):
    nc = tc.nc
    with ExitStack() as ctx:
        keep = ctx.enter_context(tc.tile_pool(name="keep", bufs=1))
        psum = ctx.enter_context(tc.psum_pool(name="psum", bufs=8))
        ctx.enter_context(tc.manual_schedule())

        xv = x.rearrange("(p j) t -> p j t", j=4)
        wv = w.rearrange("(p j) n -> p j n", j=4)
        o0 = out_0.rearrange("(a p r) t -> a p r t", a=2, r=4)
        o1 = out_1.rearrange("a p t i -> a p (t i)").bitcast(I32)
        o2 = out_2.bitcast(I32)

        codes = {}
        scales = {}
        for side, width in (("x", T), ("w", M)):
            for part in "HO":
                codes[side + part] = keep.tile([P, width], U32, align_bytes=64, name="codes_" + side + part)
                scales[side + part] = keep.tile([P, width], U8, align_bytes=64, name="scales_" + side + part)
        oscale = keep.tile([P, T], U8, align_bytes=64)
        bias = keep.tile([P, 2, 4], F32)
        warm = keep.tile([P, 8], F32)
        warm_out = keep.tile([P, 8], F32)

        nc.vector.memset(warm[:], 0.0)
        nc.scalar.activation(out=warm_out[:, 0:1], in_=warm[:, 0:1], func=GELU)
        nc.scalar.dma_start(out=bias[:], in_=b.rearrange("(a p r) -> p a r", a=2, r=4))

        xstart = [sum(XUN[:i]) for i in range(len(XUN))]
        done = {}
        raw, hi, lo, acc, res, obf, owords = {}, {}, {}, {}, {}, {}, {}

        def width_of(u):
            return XUN[int(u[1])] if u[0] == "x" else 256

        def first_col(u):
            return xstart[int(u[1])] if u[0] == "x" else 512 * int(u[1]) + 256 * int(u[2])

        def src_view(u, upper):
            if u[0] == "x":
                c0 = first_col(u)
                li = [i for i, (d0, wd) in enumerate(XLD) if d0 <= c0 < d0 + wd][0]
                t = raw["x%d" % li][:, :, c0 - XLD[li][0] : c0 - XLD[li][0] + width_of(u)]
            else:
                t = raw[u[:2]][:]
            if upper:
                t = t.bitcast(BF16)[:, :, 1::2]
            if u[0] == "x":
                return t.rearrange("p j (c i) -> p c j i", i=2)
            h = int(u[2])
            return t.rearrange("p j (m r) -> p m j r", r=4)[:, :, :, 2 * h : 2 * h + 2]

        def dst_view(u, t):
            if u[0] == "x":
                return t[:].rearrange("p (c i j) -> p c j i", i=2, j=4)
            return t[:].rearrange("p (r m j) -> p m j r", r=2, j=4)

        for task in ORDER.split():
            kind, u = task[0], task[1:]
            if kind == "L":
                if u[0] == "x":
                    c0, wd = XLD[int(u[1])]
                    raw[u] = keep.tile([P, 4, wd], F32, name="raw_" + u, align_bytes=64)
                    nc.sync.dma_start(out=raw[u][:], in_=xv[:, :, c0 : c0 + wd])
                else:
                    a = int(u[1])
                    raw[u] = keep.tile([P, 4, 512], F32, name="raw_" + u, align_bytes=64)
                    nc.sync.dma_start(out=raw[u][:], in_=wv[:, :, 512 * a : 512 * a + 512])
            elif kind == "E":
                hi[u] = keep.tile([P, 4 * width_of(u)], BF16, name="hi_" + u, align_bytes=64)
                if u in EXV:
                    nc.vector.tensor_copy(out=dst_view(u, hi[u]), in_=src_view(u, True))
                else:
                    nc.scalar.copy(out=dst_view(u, hi[u]), in_=src_view(u, True))
            elif kind == "A":
                nc.vector.tensor_scalar(
                    out=hi[u][:].bitcast(I32), in0=hi[u][:].bitcast(I32), scalar1=MASK, scalar2=None,
                    op0=mybir.AluOpType.bitwise_and,
                )
            elif kind == "C":
                lo[u] = keep.tile([P, 4 * width_of(u)], BF16, name="lo_" + u, align_bytes=64)
                nc.vector.tensor_tensor(
                    out=dst_view(u, lo[u]), in0=src_view(u, False), in1=dst_view(u, hi[u]),
                    op=mybir.AluOpType.subtract,
                )
            elif kind in "HO":
                cols = slice(first_col(u), first_col(u) + width_of(u))
                nc.vector.quantize_mx(
                    out=codes[u[0] + kind][:, cols].bitcast(FP8X4), scales=scales[u[0] + kind][:, cols],
                    in_=(hi if kind == "H" else lo)[u][:],
                )
            elif kind == "M":
                c0, n = CHUNKS[int(u[0])]
                a, r = int(u[1]), int(u[2])
                if u[:3] not in acc:
                    acc[u[:3]] = psum.tile([P, 512], F32, name="bank")
                    done[u[:3]] = 0
                mc = slice(512 * a + 128 * r, 512 * a + 128 * r + 128)
                ncol = slice(c0, c0 + n)
                pw, px = (("wH", "xH"), ("wH", "xO"), ("wO", "xH"))[int(u[3])]
                nc.tensor.matmul_mx(
                    out=acc[u[:3]][:, 0:n], lhsT=codes[pw][:, mc].bitcast(FP8X4), lhsT_scale=scales[pw][:, mc],
                    rhs=codes[px][:, ncol].bitcast(FP8X4), rhs_scale=scales[px][:, ncol],
                    start=(done[u[:3]] == 0), stop=(done[u[:3]] == 2),
                )
                done[u[:3]] += 1
            elif kind == "G":
                c0, n = CHUNKS[int(u[0])]
                a, r = int(u[1]), int(u[2])
                if u[:2] not in res:
                    res[u[:2]] = keep.tile([P, 4, n], F32, name="res_" + u[:2], align_bytes=64)
                nc.scalar.activation(out=res[u[:2]][:, r, :], in_=acc[u][:, 0:n], func=GELU, bias=bias[:, a, r : r + 1])
            elif kind == "Z":
                c0, n = CHUNKS[int(u[0])]
                a, h = int(u[1]), int(u[2])
                nc.sync.dma_start(out=o0[a, :, 2 * h : 2 * h + 2, c0 : c0 + n], in_=res[u[:2]][:, 2 * h : 2 * h + 2, :])
            elif kind == "I":
                c0, n = SEGS[int(u[0])]
                ck = [i for i, (d0, wd) in enumerate(CHUNKS) if d0 <= c0 < d0 + wd][0]
                d0 = c0 - CHUNKS[ck][0]
                obf[u] = keep.tile([P, 4 * n], BF16, name="obf_" + u, align_bytes=64)
                dst = obf[u][:].rearrange("p (c i r) -> p c r i", i=2, r=4)
                src = res["%d%s" % (ck, u[1])][:, :, d0 : d0 + n].rearrange("p r (c i) -> p c r i", i=2)
                if u in SIL:
                    nc.scalar.copy(out=dst, in_=src)
                else:
                    nc.vector.tensor_copy(out=dst, in_=src)
            elif kind == "Q":
                c0, n = SEGS[int(u[0])]
                a = int(u[1])
                owords[u] = keep.tile([P, n], U32, name="owords_" + u, align_bytes=64)
                nc.vector.quantize_mx(
                    out=owords[u][:].bitcast(FP8X4), scales=oscale[4 * a : P, c0 : c0 + n], in_=obf[u][:]
                )
            elif kind == "Y":
                c0, n = SEGS[int(u[0])]
                nc.sync.dma_start(out=o1[int(u[1]), :, c0 : c0 + n], in_=owords[u][:].bitcast(I32))
            else:
                k0, k1 = SCAL[int(u)]
                c0, c1 = SEGS[k0][0], SEGS[k1 - 1][0] + SEGS[k1 - 1][1]
                for q in range(4):
                    nc.sync.dma_start(
                        out=o2[:, 4 * q : 4 * q + 4, c0 // 4 : c1 // 4],
                        in_=oscale[32 * q : 32 * q + 8, c0:c1].bitcast(I32),
                    )
